import numpy as np
import ml_dtypes


def mxq(x, axis, fmt="e4m3"):
    dtype, down = {"e4m3": (ml_dtypes.float8_e4m3fn, 7), "e5m2": (ml_dtypes.float8_e5m2, 14)}[fmt]
    v = np.moveaxis(np.asarray(x, np.float32).astype(ml_dtypes.bfloat16).astype(np.float64), axis, -1)
    blocks = v.reshape(v.shape[:-1] + (-1, 32))
    amax = np.abs(blocks).max(-1, keepdims=True)
    byte = np.maximum(np.where(amax > 0, np.frexp(amax)[1] - 1 + 127, 0) - down, 1)
    scale = np.exp2(byte - 127.0)
    codes = (blocks / scale).astype(np.float32).astype(dtype).astype(np.float64)
    return np.moveaxis((codes * scale).reshape(v.shape), -1, axis)


WIDE = False


def mx_kscale(k):
    if not WIDE:
        return np.ones(k)
    levels = np.array([10, -10, 5, -5, 0])
    if k % 512:
        return np.exp2(np.random.permutation(np.resize(levels, k // 32))).repeat(32)
    a = np.empty((k // 512, 16))
    for p in range(k // 512):
        a[p, :8] = np.random.permutation(np.resize(levels, 8))
        for g in range(8):
            far = levels[np.abs(levels - a[p, g]) >= 10]
            a[p, g + 8] = far[np.random.randint(len(far))]
    return np.exp2(a.ravel()).repeat(32)


def f64(x):
    return np.asarray(x).astype(np.float64)


def striped(idx):
    return np.tile(idx.reshape(-1, 16).T, (8, 1)).astype(np.uint16)


def unstriped(offs):
    return offs[:16].T.reshape(-1).astype(np.int64)


def pack_weight(w):
    k, n = w.shape
    w = f64(np.asarray(w, np.float32).astype(ml_dtypes.bfloat16)).reshape(k // 32, 32, n)
    amax = np.abs(w).max(1)
    byte = np.clip(np.where(amax > 0, np.frexp(amax)[1] - 1 + 127 - 7, 1), 1, 254)
    scaled = (w * np.exp2(127.0 - byte)[:, None, :]).reshape(k, n).astype(np.float32)
    words = np.ascontiguousarray(scaled.reshape(k // 512, 128, 4, n).transpose(0, 1, 3, 2)).astype(ml_dtypes.float8_e4m3fn).view(np.uint8)
    return words, np.ascontiguousarray(byte.astype(np.uint8).reshape(k // 512, 16, n))


def unpack_weight(words, scales):
    g, p, n, _ = words.shape
    vals = np.ascontiguousarray(words).view(ml_dtypes.float8_e4m3fn).astype(np.float64) * np.repeat(np.exp2(scales.astype(np.float64) - 127.0), 8, axis=1)[..., None]
    return vals.transpose(0, 1, 3, 2).reshape(g * 512, n)


def sigmoid(v):
    return 1.0 / (1.0 + np.exp(-np.maximum(v, -700.0)))


K, T, S, N, R = 512, 1024, 512, 256, 256
P = 2 ** 7


def setup_inputs():
    n = np.random.standard_normal
    s = mx_kscale(K)[:, None]
    packed_xT = pack_weight(n((K, T)) * s)
    return {
        "x_words": packed_xT[0],
        "x_scales": packed_xT[1],
        "w1": (n((K, N)) / np.sqrt(K) / s).astype(np.float32),
        "w2": (n((K, N)) / np.sqrt(K) / s).astype(np.float32),
        "mcon": (np.random.uniform(0.2, 3.0, (N, R))).astype(np.float32),
        "lfc": (np.tile(-np.random.uniform(0.3, 1.2, S), (P, 1))).astype(np.float32),
        "wor": (np.random.uniform(0.2, 0.8, (N, 1))).astype(np.float32),
        "offs": striped(np.random.permutation(T)[:S]),
        "bath": striped(np.random.permutation(np.concatenate([np.arange(R), np.random.randint(0, R, S - R)]))),
    }


def reference(x_words, x_scales, w1, w2, mcon, lfc, wor, offs, bath):
    xq = unpack_weight(x_words, x_scales)[:, unstriped(offs)]
    yi = mxq(f64(w2), 0, "e4m3").T @ xq
    yo = mxq(f64(w1), 0, "e4m3").T @ xq
    mb = f64(mcon)[:, unstriped(bath)]
    lpr = 0.8 * (yo - yi) + np.log(mb)
    lf = f64(lfc)[:1] / (((lpr - 0.4) / (-1.0 * (0.5 * f64(lfc)[:1]) + 1.0)) ** 2 + 1.0)
    lk = 0.8 * yi + lpr - (np.log(np.exp(lpr) + 1.0)) + lf
    return np.exp(0.5 * lk) - (f64(wor) * (sigmoid(lpr) * (lf + 1.0)))

@@ -1,0 +1,256 @@
+import math
+from contextlib import ExitStack
+
+import concourse.mybir as mybir
+from concourse.masks import make_identity
+
+K, T, S, N, R = 512, 1024, 512, 256, 256
+FLOPS = 2 * 2 * K * S * N
+
+F32 = mybir.dt.float32
+BF16 = mybir.dt.bfloat16
+I32 = mybir.dt.int32
+U32 = mybir.dt.uint32
+U16 = mybir.dt.uint16
+U8 = mybir.dt.uint8
+FP8X4 = mybir.dt.float8_e4m3fn_x4
+ALU = mybir.AluOpType
+ACT = mybir.ActivationFunctionType
+
+P = 128
+PACK = 4
+HALF = S // 2
+MB = N // P
+JB = S // P
+SPARE = 8
+TINY = 1e-14
+
+
+def tile_picked_ytroef_root_p_kernel(
+    tc, x_words, x_scales, w1, w2, mcon, lfc, wor, offs, bath, out
+):
+    nc = tc.nc
+    with ExitStack() as ctx:
+        keep = ctx.enter_context(tc.tile_pool(name="keep", bufs=1))
+        psum = ctx.enter_context(tc.psum_pool(name="psum", bufs=1))
+
+        def sb(name, shape, dtype, tag=""):
+            return keep.tile(shape, dtype, name=name, tag=tag, align_bytes=64)
+
+        def bank(name, tag):
+            return psum.tile([P, 2 * N], F32, name=name, tag=tag)
+
+        offs_t = keep.tile([P, S // 16], U16, name="offs_t")
+        bath_t = keep.tile([P, S // 16], U16, name="bath_t")
+
+        one = sb("one", [P, 1], F32)
+        warm = sb("warm", [P, 1], F32)
+        nc.vector.memset(one[:], 1.0)
+        nc.scalar.activation(out=warm[:], in_=one[:], func=ACT.Ln)
+
+        conc = [sb("conc%d" % b, [P, R + SPARE], F32) for b in range(MB)]
+        scale_win = sb("scale_win", [P, T], U8)
+        nc.gpsimd.memset(scale_win[:].bitcast(I32), 0)
+        for b in range(MB):
+            nc.gpsimd.memset(conc[b][:, R:], 0.0)
+        ident = sb("ident", [P, P], F32)
+        make_identity(nc, ident[:])
+
+        word_win = sb("word_win", [P, T], I32)
+        w1_raw = sb("w1_raw", [P, PACK * N], F32)
+        stage = sb("stage", [P, S + PACK * N], F32)
+        w_raw = [t.rearrange("p (t n) -> p t n", t=PACK) for t in (w1_raw[:], stage[:, S:])]
+        cen = sb("cen", [P, JB], F32)
+        wgt = sb("wgt", [P, MB], F32)
+
+        nc.sync.dma_start(conc[0][:, :R], mcon[0:P, :])
+        nc.sync.dma_start(bath_t[:], bath)
+        nc.sync.dma_start(conc[1][:, :R], mcon[P : 2 * P, :])
+        nc.sync.dma_start(offs_t[:], offs)
+        nc.sync.dma_start(word_win[:], x_words[0].rearrange("p c r -> p (c r)").bitcast(I32))
+        nc.sync.dma_start(w_raw[0], w1.rearrange("(p t) n -> p t n", t=PACK))
+        for q in range(4):
+            nc.sync.dma_start(
+                scale_win[32 * q : 32 * q + 4, :].bitcast(I32), x_scales[0, 4 * q : 4 * q + 4, :].bitcast(I32)
+            )
+        nc.sync.dma_start(w_raw[1], w2.rearrange("(p t) n -> p t n", t=PACK))
+        with nc.allow_non_contiguous_dma(reason="one value a partition"):
+            nc.sync.dma_start(cen[:], lfc[0, :].rearrange("(b p) -> p b", p=P))
+            nc.sync.dma_start(wgt[:], wor.rearrange("(b p) o -> p (b o)", p=P))
+
+        w_codes = [sb("w_codes%d" % i, [P, N], U32) for i in range(2)]
+        w_scales = [sb("w_scales%d" % i, [P, N], U8) for i in range(2)]
+        w_bf = [sb("w_bf%d" % i, [P, N, PACK], BF16, "woven%d" % i) for i in range(2)]
+
+        def weave(i):
+            nc.scalar.copy(
+                out=w_bf[i][:].rearrange("p (c i) t -> p c t i", i=4),
+                in_=w_raw[i].rearrange("p t (c i) -> p c t i", i=4),
+            )
+
+        weave(0)
+        weave(1)
+        lt = stage[:, : MB * S].rearrange("p (b j m) -> p b j m", b=MB, j=JB)
+        picked = [[sb("picked%d_%d" % (b, h), [P, HALF], F32) for h in range(2)] for b in range(MB)]
+        for b in range(MB):
+            for h in range(2):
+                nc.vector.tensor_copy(out=picked[b][h][:], in_=conc[b][:].indirect(bath_t[:, 16 * h : 16 * h + 16]))
+        for b in range(MB):
+            turned = bank("turned%d" % b, "a%d" % b)
+            for jb in range(JB):
+                nc.tensor.transpose(
+                    turned[:, jb * P : (jb + 1) * P], picked[b][jb // 2][:, (jb % 2) * P : (jb % 2 + 1) * P], ident[:]
+                )
+            nc.scalar.activation(
+                out=stage[:, b * S : (b + 1) * S],
+                in_=turned[:],
+                func=ACT.Ln,
+                scale=math.exp(-0.4),
+            )
+
+        x_codes, x_bytes = [], []
+
+        def pick_words(h, tag):
+            x_codes.append(sb("x_codes%d" % h, [P, HALF], U32, tag))
+            nc.vector.tensor_copy(
+                out=x_codes[h][:], in_=word_win[:].bitcast(U32).indirect(offs_t[:, 16 * h : 16 * h + 16])
+            )
+
+        def pick_bytes(h, tag):
+            x_bytes.append(sb("x_bytes%d" % h, [P, HALF], U8, tag))
+            nc.vector.tensor_copy(out=x_bytes[h][:], in_=scale_win[:].indirect(offs_t[:, 16 * h : 16 * h + 16]))
+
+        def quantise(i):
+            nc.vector.quantize_mx(
+                out=w_codes[i][:].bitcast(FP8X4), scales=w_scales[i][:], in_=w_bf[i][:].rearrange("p n t -> p (n t)")
+            )
+
+        pick_words(0, "")
+        pick_bytes(0, "")
+        quantise(0)
+        pick_words(1, "woven0")
+        quantise(1)
+        pick_bytes(1, "woven1")
+
+        y = [[bank("y%d_%d" % (i, h), "y%d_%d" % (i, h)) for h in range(2)] for i in range(2)]
+        for h in range(2):
+            for i in range(2):
+                for jl in range(2):
+                    cols = slice(jl * P, (jl + 1) * P)
+                    nc.tensor.matmul_mx(
+                        out=y[i][h][:, jl * N : (jl + 1) * N],
+                        lhsT=x_codes[h][:, cols].bitcast(FP8X4),
+                        lhsT_scale=x_bytes[h][:, cols],
+                        rhs=w_codes[i][:].bitcast(FP8X4),
+                        rhs_scale=w_scales[i][:],
+                        start=True,
+                        stop=True,
+                    )
+
+        wid = sb("wid", [P, JB], F32)
+        wid2 = sb("wid2", [P, JB], F32)
+        cw2 = sb("cw2", [P, JB], F32)
+        nc.gpsimd.tensor_scalar(out=wid[:], in0=cen[:], scalar1=-0.5, scalar2=1.0, op0=ALU.mult, op1=ALU.add)
+        nc.gpsimd.tensor_tensor(out=wid2[:], in0=wid[:], in1=wid[:], op=ALU.mult)
+        nc.gpsimd.tensor_tensor(out=cw2[:], in0=wid2[:], in1=cen[:], op=ALU.mult)
+
+        def halves(name):
+            return [sb("%s%d" % (name, h), [P, 2 * N], F32) for h in range(2)]
+
+        low, gap, far, sq, lfar, lmin, rec, lf1, near, root, res = (
+            halves(n) for n in ("low", "gap", "far", "sq", "lfar", "lmin", "rec", "lf1", "near", "root", "res")
+        )
+        den = sb("den", [P, 2 * N], F32)
+        lden = sb("lden", [P, 2 * N], F32)
+        pair = sb("pair", [P, N], F32)
+        inv = sb("inv", [P, N], F32)
+        blk = [slice(jl * N, (jl + 1) * N) for jl in range(2)]
+
+        for h in range(2):
+            for jl in range(2):
+                nc.vector.scalar_tensor_tensor(
+                    out=low[h][:, blk[jl]].rearrange("p (b m) -> p b m", b=MB),
+                    in0=y[0][h][:, blk[jl]].rearrange("p (b m) -> p b m", b=MB), scalar=0.8,
+                    in1=lt[:, :, 2 * h + jl, :], op0=ALU.mult, op1=ALU.add,
+                )
+            for jl in range(2):
+                nc.vector.scalar_tensor_tensor(
+                    out=gap[h][:, blk[jl]], in0=y[1][h][:, blk[jl]], scalar=0.8, in1=low[h][:, blk[jl]],
+                    op0=ALU.mult, op1=ALU.subtract,
+                )
+        nc.scalar.activation(out=far[0][:], in_=gap[0][:], func=ACT.Sigmoid, bias=-0.4)
+        nc.scalar.activation(out=sq[0][:], in_=gap[0][:], func=ACT.Square)
+        nc.scalar.activation(out=far[1][:], in_=gap[1][:], func=ACT.Sigmoid, bias=-0.4)
+
+        for jl in range(2):
+            nc.vector.tensor_scalar(
+                out=den[:, blk[jl]], in0=sq[0][:, blk[jl]], scalar1=wid2[:, jl : jl + 1], scalar2=None, op0=ALU.add
+            )
+        nc.vector.tensor_tensor(out=sq[1][:], in0=gap[1][:], in1=gap[1][:], op=ALU.mult)
+        nc.vector.tensor_tensor(out=pair[:], in0=den[:, blk[0]], in1=den[:, blk[1]], op=ALU.mult)
+        nc.vector.reciprocal(out=inv[:], in_=pair[:])
+
+        for h in range(2):
+            nc.scalar.activation(out=lfar[h][:], in_=far[h][:], func=ACT.Ln, scale=math.exp(0.4), bias=TINY)
+        for jl in range(2):
+            nc.scalar.activation(
+                out=lden[:, blk[jl]], in_=sq[1][:, blk[jl]], func=ACT.Ln, bias=wid2[:, 2 + jl : 3 + jl]
+            )
+        for jl in range(2):
+            nc.scalar.activation(out=rec[1][:, blk[jl]], in_=lden[:, blk[jl]], func=ACT.Exp, scale=-1.0)
+
+        zb = [bank("z%d" % h, "z%d" % h) for h in range(2)]
+        hb = [bank("h%d" % h, "a%d" % h) for h in range(2)]
+
+        def turn(dst, src, first, last):
+            for jl in range(2):
+                for b in range(MB):
+                    nc.tensor.matmul(
+                        out=dst[:, b * HALF + jl * P : b * HALF + (jl + 1) * P],
+                        lhsT=src[:, jl * N + b * P : jl * N + (b + 1) * P],
+                        rhs=ident[:],
+                        is_transpose=True,
+                        start=first and jl == 0 and b == 0,
+                        stop=last and jl == 1 and b == MB - 1,
+                    )
+
+        def broaden(h):
+            for jl in range(2):
+                jb = 2 * h + jl
+                nc.vector.tensor_scalar(
+                    out=lf1[h][:, blk[jl]], in0=rec[h][:, blk[jl]], scalar1=cw2[:, jb : jb + 1], scalar2=1.0,
+                    op0=ALU.mult, op1=ALU.add,
+                )
+
+        def floor(h):
+            nc.vector.tensor_tensor(out=lmin[h][:], in0=lfar[h][:], in1=gap[h][:], op=ALU.min)
+
+        def nearness(h):
+            for jl in range(2):
+                nc.vector.scalar_tensor_tensor(
+                    out=near[h][:, blk[jl]], in0=far[h][:, blk[jl]], scalar=1.0, in1=lf1[h][:, blk[jl]],
+                    op0=ALU.subtract, op1=ALU.mult,
+                )
+            turn(hb[h], near[h], True, True)
+
+        for h in range(2):
+            turn(zb[h], low[h], True, False)
+        for h in range(2):
+            floor(h)
+            turn(zb[h], lmin[h], False, False)
+        for jl in range(2):
+            nc.vector.tensor_tensor(out=rec[0][:, blk[jl]], in0=inv[:], in1=den[:, blk[1 - jl]], op=ALU.mult)
+        for h in range(2):
+            broaden(h)
+            turn(zb[h], lf1[h], False, True)
+            nearness(h)
+
+        for h in range(2):
+            nc.scalar.activation(out=root[h][:], in_=zb[h][:], func=ACT.Exp, scale=0.5, bias=-0.5)
+            for b in range(MB):
+                cols = slice(b * HALF, (b + 1) * HALF)
+                nc.vector.scalar_tensor_tensor(
+                    out=res[h][:, cols], in0=hb[h][:, cols], scalar=wgt[:, b : b + 1], in1=root[h][:, cols],
+                    op0=ALU.mult, op1=ALU.add,
+                )
+                nc.sync.dma_start(out[b * P : (b + 1) * P, h * HALF : (h + 1) * HALF], res[h][:, cols])

@@ -57,9 +57,7 @@ def tile_picked_ytroef_root_p_kernel(
         make_identity(nc, ident[:])
 
         word_win = sb("word_win", [P, T], I32)
-        w1_raw = sb("w1_raw", [P, PACK * N], F32)
-        stage = sb("stage", [P, S + PACK * N], F32)
-        w_raw = [t.rearrange("p (t n) -> p t n", t=PACK) for t in (w1_raw[:], stage[:, S:])]
+        w_raw = [sb("w_raw%d" % i, [P, PACK, N], F32)[:] for i in range(2)]
         cen = sb("cen", [P, JB], F32)
         wgt = sb("wgt", [P, MB], F32)
 
@@ -90,7 +88,7 @@ def tile_picked_ytroef_root_p_kernel(
 
         weave(0)
         weave(1)
-        lt = stage[:, : MB * S].rearrange("p (b j m) -> p b j m", b=MB, j=JB)
+        lt = w_raw[1]
         picked = [[sb("picked%d_%d" % (b, h), [P, HALF], F32) for h in range(2)] for b in range(MB)]
         for b in range(MB):
             for h in range(2):
@@ -102,8 +100,8 @@ def tile_picked_ytroef_root_p_kernel(
                     turned[:, jb * P : (jb + 1) * P], picked[b][jb // 2][:, (jb % 2) * P : (jb % 2 + 1) * P], ident[:]
                 )
             nc.scalar.activation(
-                out=stage[:, b * S : (b + 1) * S],
-                in_=turned[:],
+                out=lt[:, :, b * P : (b + 1) * P],
+                in_=turned[:].rearrange("p (j m) -> p j m", j=JB),
                 func=ACT.Ln,
                 scale=math.exp(-0.4),
             )
@@ -157,47 +155,55 @@ def tile_picked_ytroef_root_p_kernel(
         def halves(name):
             return [sb("%s%d" % (name, h), [P, 2 * N], F32) for h in range(2)]
 
-        low, gap, far, sq, lfar, lmin, rec, lf1, near, root, res = (
-            halves(n) for n in ("low", "gap", "far", "sq", "lfar", "lmin", "rec", "lf1", "near", "root", "res")
-        )
+        low, gap, far, lfar, lmin, near = (halves(n) for n in ("low", "gap", "far", "lfar", "lmin", "near"))
+        lf = [lfar[1], lfar[0]]
+        side = sb("side", [P, 4 * N], F32)
+        sq, farm = side[:, : 2 * N], side[:, 2 * N :]
+        sq0 = [side[:, 3 * N // 2 : 5 * N // 2], side[:, :N]]
         den = sb("den", [P, 2 * N], F32)
         lden = sb("lden", [P, 2 * N], F32)
+        rec = sb("rec", [P, 2 * N], F32)
+        root = [lden, sb("root1", [P, 2 * N], F32)]
+        res = [rec, sb("res1", [P, 2 * N], F32)]
         pair = sb("pair", [P, N], F32)
         inv = sb("inv", [P, N], F32)
         blk = [slice(jl * N, (jl + 1) * N) for jl in range(2)]
 
         for h in range(2):
-            for jl in range(2):
-                nc.vector.scalar_tensor_tensor(
-                    out=low[h][:, blk[jl]].rearrange("p (b m) -> p b m", b=MB),
-                    in0=y[0][h][:, blk[jl]].rearrange("p (b m) -> p b m", b=MB), scalar=0.8,
-                    in1=lt[:, :, 2 * h + jl, :], op0=ALU.mult, op1=ALU.add,
-                )
-            for jl in range(2):
-                nc.vector.scalar_tensor_tensor(
-                    out=gap[h][:, blk[jl]], in0=y[1][h][:, blk[jl]], scalar=0.8, in1=low[h][:, blk[jl]],
-                    op0=ALU.mult, op1=ALU.subtract,
-                )
-        nc.scalar.activation(out=far[0][:], in_=gap[0][:], func=ACT.Sigmoid, bias=-0.4)
-        nc.scalar.activation(out=sq[0][:], in_=gap[0][:], func=ACT.Square)
-        nc.scalar.activation(out=far[1][:], in_=gap[1][:], func=ACT.Sigmoid, bias=-0.4)
-
-        for jl in range(2):
-            nc.vector.tensor_scalar(
-                out=den[:, blk[jl]], in0=sq[0][:, blk[jl]], scalar1=wid2[:, jl : jl + 1], scalar2=None, op0=ALU.add
+            nc.vector.scalar_tensor_tensor(
+                out=low[h][:], in0=y[0][h][:], scalar=0.8,
+                in1=lt[:, 2 * h : 2 * h + 2, :].rearrange("p j m -> p (j m)"), op0=ALU.mult, op1=ALU.add,
             )
-        nc.vector.tensor_tensor(out=sq[1][:], in0=gap[1][:], in1=gap[1][:], op=ALU.mult)
-        nc.vector.tensor_tensor(out=pair[:], in0=den[:, blk[0]], in1=den[:, blk[1]], op=ALU.mult)
+        for h in range(2):
+            nc.vector.scalar_tensor_tensor(
+                out=gap[h][:], in0=y[1][h][:], scalar=0.8, in1=low[h][:], op0=ALU.mult, op1=ALU.subtract
+            )
+        for h in range(2):
+            nc.scalar.activation(out=far[h][:], in_=gap[h][:], func=ACT.Sigmoid, bias=-0.4)
+
+        for jl in (1, 0):
+            nc.vector.tensor_tensor(
+                out=sq0[jl], in0=gap[0][:, blk[jl]], in1=gap[0][:, blk[jl]], op=ALU.mult
+            )
+        for jl in (1, 0):
+            nc.vector.tensor_scalar(
+                out=den[:, blk[jl]], in0=sq0[jl], scalar1=wid2[:, jl : jl + 1], scalar2=None, op0=ALU.add
+            )
+        nc.vector.scalar_tensor_tensor(
+            out=pair[:], in0=sq0[0], scalar=wid2[:, 0:1], in1=den[:, blk[1]], op0=ALU.add, op1=ALU.mult
+        )
         nc.vector.reciprocal(out=inv[:], in_=pair[:])
+        nc.gpsimd.tensor_tensor(out=sq, in0=gap[1][:], in1=gap[1][:], op=ALU.mult)
+        nc.gpsimd.tensor_scalar(out=farm, in0=far[0][:], scalar1=1.0, scalar2=-1.0, op0=ALU.mult, op1=ALU.add)
 
         for h in range(2):
             nc.scalar.activation(out=lfar[h][:], in_=far[h][:], func=ACT.Ln, scale=math.exp(0.4), bias=TINY)
         for jl in range(2):
             nc.scalar.activation(
-                out=lden[:, blk[jl]], in_=sq[1][:, blk[jl]], func=ACT.Ln, bias=wid2[:, 2 + jl : 3 + jl]
+                out=lden[:, blk[jl]], in_=sq[:, blk[jl]], func=ACT.Ln, bias=wid2[:, 2 + jl : 3 + jl]
             )
         for jl in range(2):
-            nc.scalar.activation(out=rec[1][:, blk[jl]], in_=lden[:, blk[jl]], func=ACT.Exp, scale=-1.0)
+            nc.scalar.activation(out=rec[:, blk[jl]], in_=lden[:, blk[jl]], func=ACT.Exp, scale=-1.0)
 
         zb = [bank("z%d" % h, "z%d" % h) for h in range(2)]
         hb = [bank("h%d" % h, "a%d" % h) for h in range(2)]
@@ -214,39 +220,38 @@ def tile_picked_ytroef_root_p_kernel(
                         stop=last and jl == 1 and b == MB - 1,
                     )
 
-        def broaden(h):
-            for jl in range(2):
-                jb = 2 * h + jl
-                nc.vector.tensor_scalar(
-                    out=lf1[h][:, blk[jl]], in0=rec[h][:, blk[jl]], scalar1=cw2[:, jb : jb + 1], scalar2=1.0,
-                    op0=ALU.mult, op1=ALU.add,
-                )
-
-        def floor(h):
-            nc.vector.tensor_tensor(out=lmin[h][:], in0=lfar[h][:], in1=gap[h][:], op=ALU.min)
-
-        def nearness(h):
-            for jl in range(2):
-                nc.vector.scalar_tensor_tensor(
-                    out=near[h][:, blk[jl]], in0=far[h][:, blk[jl]], scalar=1.0, in1=lf1[h][:, blk[jl]],
-                    op0=ALU.subtract, op1=ALU.mult,
-                )
-            turn(hb[h], near[h], True, True)
-
         for h in range(2):
             turn(zb[h], low[h], True, False)
         for h in range(2):
-            floor(h)
+            nc.vector.tensor_tensor(out=lmin[h][:], in0=lfar[h][:], in1=gap[h][:], op=ALU.min)
             turn(zb[h], lmin[h], False, False)
         for jl in range(2):
-            nc.vector.tensor_tensor(out=rec[0][:, blk[jl]], in0=inv[:], in1=den[:, blk[1 - jl]], op=ALU.mult)
-        for h in range(2):
-            broaden(h)
-            turn(zb[h], lf1[h], False, True)
-            nearness(h)
+            nc.vector.scalar_tensor_tensor(
+                out=lf[0][:, blk[jl]], in0=inv[:], scalar=cw2[:, jl : jl + 1], in1=den[:, blk[1 - jl]],
+                op0=ALU.mult, op1=ALU.mult,
+            )
+        turn(zb[0], lf[0], False, True)
+        for jl in range(2):
+            nc.vector.scalar_tensor_tensor(
+                out=near[0][:, blk[jl]], in0=lf[0][:, blk[jl]], scalar=1.0, in1=farm[:, blk[jl]],
+                op0=ALU.add, op1=ALU.mult,
+            )
+        turn(hb[0], near[0], True, True)
+        for jl in range(2):
+            nc.vector.tensor_scalar(
+                out=lf[1][:, blk[jl]], in0=rec[:, blk[jl]], scalar1=cw2[:, 2 + jl : 3 + jl], scalar2=1.0,
+                op0=ALU.mult, op1=ALU.add,
+            )
+        turn(zb[1], lf[1], False, True)
+        for jl in range(2):
+            nc.vector.scalar_tensor_tensor(
+                out=near[1][:, blk[jl]], in0=far[1][:, blk[jl]], scalar=1.0, in1=lf[1][:, blk[jl]],
+                op0=ALU.subtract, op1=ALU.mult,
+            )
+        turn(hb[1], near[1], True, True)
 
         for h in range(2):
-            nc.scalar.activation(out=root[h][:], in_=zb[h][:], func=ACT.Exp, scale=0.5, bias=-0.5)
+            nc.scalar.activation(out=root[h][:], in_=zb[h][:], func=ACT.Exp, scale=0.5, bias=-0.5 * h)
             for b in range(MB):
                 cols = slice(b * HALF, (b + 1) * HALF)
                 nc.vector.scalar_tensor_tensor(

@@ -22,7 +22,7 @@ PACK = 4
 HALF = S // 2
 MB = N // P
 JB = S // P
-SPARE = 8
+SPARE = 96
 TINY = 1e-14
 
 
@@ -48,11 +48,10 @@ def tile_picked_ytroef_root_p_kernel(
         nc.vector.memset(one[:], 1.0)
         nc.scalar.activation(out=warm[:], in_=one[:], func=ACT.Ln)
 
-        conc = [sb("conc%d" % b, [P, R + SPARE], F32) for b in range(MB)]
+        conc = sb("conc", [P, MB * R + SPARE], F32)
         scale_win = sb("scale_win", [P, T], U8)
         nc.gpsimd.memset(scale_win[:].bitcast(I32), 0)
-        for b in range(MB):
-            nc.gpsimd.memset(conc[b][:, R:], 0.0)
+        nc.gpsimd.memset(conc[:, MB * R :], 0.0)
         ident = sb("ident", [P, P], F32)
         make_identity(nc, ident[:])
 
@@ -61,16 +60,17 @@ def tile_picked_ytroef_root_p_kernel(
         cen = sb("cen", [P, JB], F32)
         wgt = sb("wgt", [P, MB], F32)
 
-        nc.sync.dma_start(conc[0][:, :R], mcon[0:P, :])
+        nc.sync.dma_start(
+            conc[:, : MB * R].rearrange("p (b r) -> p b r", b=MB), mcon.rearrange("(b p) r -> p b r", p=P)
+        )
         nc.sync.dma_start(bath_t[:], bath)
-        nc.sync.dma_start(conc[1][:, :R], mcon[P : 2 * P, :])
-        nc.sync.dma_start(offs_t[:], offs)
-        nc.sync.dma_start(word_win[:], x_words[0].rearrange("p c r -> p (c r)").bitcast(I32))
-        nc.sync.dma_start(w_raw[0], w1.rearrange("(p t) n -> p t n", t=PACK))
         for q in range(4):
             nc.sync.dma_start(
                 scale_win[32 * q : 32 * q + 4, :].bitcast(I32), x_scales[0, 4 * q : 4 * q + 4, :].bitcast(I32)
             )
+        nc.sync.dma_start(w_raw[0], w1.rearrange("(p t) n -> p t n", t=PACK))
+        nc.sync.dma_start(word_win[:], x_words[0].rearrange("p c r -> p (c r)").bitcast(I32))
+        nc.sync.dma_start(offs_t[:], offs)
         nc.sync.dma_start(w_raw[1], w2.rearrange("(p t) n -> p t n", t=PACK))
         with nc.allow_non_contiguous_dma(reason="one value a partition"):
             nc.sync.dma_start(cen[:], lfc[0, :].rearrange("(b p) -> p b", p=P))
@@ -87,12 +87,11 @@ def tile_picked_ytroef_root_p_kernel(
             )
 
         weave(0)
-        weave(1)
-        lt = w_raw[1]
+        lt = w_raw[0]
         picked = [[sb("picked%d_%d" % (b, h), [P, HALF], F32) for h in range(2)] for b in range(MB)]
         for b in range(MB):
             for h in range(2):
-                nc.vector.tensor_copy(out=picked[b][h][:], in_=conc[b][:].indirect(bath_t[:, 16 * h : 16 * h + 16]))
+                nc.vector.tensor_copy(out=picked[b][h][:], in_=conc[:, b * R : (b + 1) * R + SPARE].indirect(bath_t[:, 16 * h : 16 * h + 16]))
         for b in range(MB):
             turned = bank("turned%d" % b, "a%d" % b)
             for jb in range(JB):
@@ -106,6 +105,7 @@ def tile_picked_ytroef_root_p_kernel(
                 scale=math.exp(-0.4),
             )
 
+        weave(1)
         x_codes, x_bytes = [], []
 
         def pick_words(h, tag):
@@ -127,12 +127,12 @@ def tile_picked_ytroef_root_p_kernel(
         pick_bytes(0, "")
         quantise(0)
         pick_words(1, "woven0")
+        pick_bytes(1, "")
         quantise(1)
-        pick_bytes(1, "woven1")
 
         y = [[bank("y%d_%d" % (i, h), "y%d_%d" % (i, h)) for h in range(2)] for i in range(2)]
-        for h in range(2):
-            for i in range(2):
+        for i in range(2):
+            for h in range(2):
                 for jl in range(2):
                     cols = slice(jl * P, (jl + 1) * P)
                     nc.tensor.matmul_mx(
@@ -174,12 +174,12 @@ def tile_picked_ytroef_root_p_kernel(
                 out=low[h][:], in0=y[0][h][:], scalar=0.8,
                 in1=lt[:, 2 * h : 2 * h + 2, :].rearrange("p j m -> p (j m)"), op0=ALU.mult, op1=ALU.add,
             )
-        for h in range(2):
+        for h, cols in ((0, slice(0, 2 * N)), (1, blk[0]), (1, blk[1])):
             nc.vector.scalar_tensor_tensor(
-                out=gap[h][:], in0=y[1][h][:], scalar=0.8, in1=low[h][:], op0=ALU.mult, op1=ALU.subtract
+                out=gap[h][:, cols], in0=y[1][h][:, cols], scalar=0.8, in1=low[h][:, cols],
+                op0=ALU.mult, op1=ALU.subtract,
             )
-        for h in range(2):
-            nc.scalar.activation(out=far[h][:], in_=gap[h][:], func=ACT.Sigmoid, bias=-0.4)
+            nc.scalar.activation(out=far[h][:, cols], in_=gap[h][:, cols], func=ACT.Sigmoid, bias=-0.4)
 
         for jl in (1, 0):
             nc.vector.tensor_tensor(

@@ -44,9 +44,9 @@ def tile_picked_ytroef_root_p_kernel(
         bath_t = keep.tile([P, S // 16], U16, name="bath_t")
 
         one = sb("one", [P, 1], F32)
-        warm = sb("warm", [P, 1], F32)
+        shift = sb("shift", [P, 1], F32)
         nc.vector.memset(one[:], 1.0)
-        nc.scalar.activation(out=warm[:], in_=one[:], func=ACT.Ln)
+        nc.scalar.activation(out=shift[:], in_=one[:], func=ACT.Ln, scale=math.exp(-0.4))
 
         conc = sb("conc", [P, MB * R + SPARE], F32)
         scale_win = sb("scale_win", [P, T], U8)
@@ -145,20 +145,16 @@ def tile_picked_ytroef_root_p_kernel(
                         stop=True,
                     )
 
-        wid = sb("wid", [P, JB], F32)
         wid2 = sb("wid2", [P, JB], F32)
-        cw2 = sb("cw2", [P, JB], F32)
-        nc.gpsimd.tensor_scalar(out=wid[:], in0=cen[:], scalar1=-0.5, scalar2=1.0, op0=ALU.mult, op1=ALU.add)
-        nc.gpsimd.tensor_tensor(out=wid2[:], in0=wid[:], in1=wid[:], op=ALU.mult)
-        nc.gpsimd.tensor_tensor(out=cw2[:], in0=wid2[:], in1=cen[:], op=ALU.mult)
+        nc.scalar.activation(out=wid2[:], in_=cen[:], func=ACT.Square, scale=-0.5, bias=1.0)
 
         def halves(name):
             return [sb("%s%d" % (name, h), [P, 2 * N], F32) for h in range(2)]
 
         low, gap, far, lfar, lmin, near = (halves(n) for n in ("low", "gap", "far", "lfar", "lmin", "near"))
         lf = [lfar[1], lfar[0]]
-        side = sb("side", [P, 4 * N], F32)
-        sq, farm = side[:, : 2 * N], side[:, 2 * N :]
+        side = sb("side", [P, 4 * N + 8], F32)
+        sq, cw2, farm = side[:, : 2 * N], side[:, 2 * N : 2 * N + JB], side[:, 2 * N + 8 :]
         sq0 = [side[:, 3 * N // 2 : 5 * N // 2], side[:, :N]]
         den = sb("den", [P, 2 * N], F32)
         lden = sb("lden", [P, 2 * N], F32)
@@ -179,7 +175,7 @@ def tile_picked_ytroef_root_p_kernel(
                 out=gap[h][:, cols], in0=y[1][h][:, cols], scalar=0.8, in1=low[h][:, cols],
                 op0=ALU.mult, op1=ALU.subtract,
             )
-            nc.scalar.activation(out=far[h][:, cols], in_=gap[h][:, cols], func=ACT.Sigmoid, bias=-0.4)
+            nc.scalar.activation(out=far[h][:, cols], in_=gap[h][:, cols], func=ACT.Sigmoid, bias=shift[:])
 
         for jl in (1, 0):
             nc.vector.tensor_tensor(
@@ -194,6 +190,7 @@ def tile_picked_ytroef_root_p_kernel(
         )
         nc.vector.reciprocal(out=inv[:], in_=pair[:])
         nc.gpsimd.tensor_tensor(out=sq, in0=gap[1][:], in1=gap[1][:], op=ALU.mult)
+        nc.gpsimd.tensor_tensor(out=cw2, in0=wid2[:], in1=cen[:], op=ALU.mult)
         nc.gpsimd.tensor_scalar(out=farm, in0=far[0][:], scalar1=1.0, scalar2=-1.0, op0=ALU.mult, op1=ALU.add)
 
         for h in range(2):
@@ -205,57 +202,61 @@ def tile_picked_ytroef_root_p_kernel(
         for jl in range(2):
             nc.scalar.activation(out=rec[:, blk[jl]], in_=lden[:, blk[jl]], func=ACT.Exp, scale=-1.0)
 
-        zb = [bank("z%d" % h, "z%d" % h) for h in range(2)]
-        hb = [bank("h%d" % h, "a%d" % h) for h in range(2)]
+        z0, h0 = bank("z0", "z0"), bank("h0", "a0")
+        zb = [[z0[:, blk[b]] for b in range(MB)], [bank("z1_%d" % b, t)[:, :HALF] for b, t in enumerate(("z1", "a1"))]]
+        hb = [[h0[:, blk[b]] for b in range(MB)], [bank("h1_%d" % b, "y0_%d" % b)[:, :HALF] for b in range(MB)]]
 
-        def turn(dst, src, first, last):
+        def turn(dst, h, src, first, last):
             for jl in range(2):
                 for b in range(MB):
+                    opens = jl == 0 and (h == 1 or b == 0)
+                    closes = jl == 1 and (h == 1 or b == MB - 1)
                     nc.tensor.matmul(
-                        out=dst[:, b * HALF + jl * P : b * HALF + (jl + 1) * P],
+                        out=dst[h][b][:, jl * P : (jl + 1) * P],
                         lhsT=src[:, jl * N + b * P : jl * N + (b + 1) * P],
                         rhs=ident[:],
                         is_transpose=True,
-                        start=first and jl == 0 and b == 0,
-                        stop=last and jl == 1 and b == MB - 1,
+                        start=first and opens,
+                        stop=last and closes,
                     )
 
         for h in range(2):
-            turn(zb[h], low[h], True, False)
+            turn(zb, h, low[h], True, False)
         for h in range(2):
             nc.vector.tensor_tensor(out=lmin[h][:], in0=lfar[h][:], in1=gap[h][:], op=ALU.min)
-            turn(zb[h], lmin[h], False, False)
+            turn(zb, h, lmin[h], False, False)
         for jl in range(2):
             nc.vector.scalar_tensor_tensor(
                 out=lf[0][:, blk[jl]], in0=inv[:], scalar=cw2[:, jl : jl + 1], in1=den[:, blk[1 - jl]],
                 op0=ALU.mult, op1=ALU.mult,
             )
-        turn(zb[0], lf[0], False, True)
+        turn(zb, 0, lf[0], False, True)
         for jl in range(2):
             nc.vector.scalar_tensor_tensor(
                 out=near[0][:, blk[jl]], in0=lf[0][:, blk[jl]], scalar=1.0, in1=farm[:, blk[jl]],
                 op0=ALU.add, op1=ALU.mult,
             )
-        turn(hb[0], near[0], True, True)
+        turn(hb, 0, near[0], True, True)
         for jl in range(2):
             nc.vector.tensor_scalar(
                 out=lf[1][:, blk[jl]], in0=rec[:, blk[jl]], scalar1=cw2[:, 2 + jl : 3 + jl], scalar2=1.0,
                 op0=ALU.mult, op1=ALU.add,
             )
-        turn(zb[1], lf[1], False, True)
+        turn(zb, 1, lf[1], False, True)
         for jl in range(2):
             nc.vector.scalar_tensor_tensor(
                 out=near[1][:, blk[jl]], in0=far[1][:, blk[jl]], scalar=1.0, in1=lf[1][:, blk[jl]],
                 op0=ALU.subtract, op1=ALU.mult,
             )
-        turn(hb[1], near[1], True, True)
+        turn(hb, 1, near[1], True, True)
 
+        nc.scalar.activation(out=root[0][:], in_=z0[:], func=ACT.Exp, scale=0.5)
+        for b in range(MB):
+            nc.scalar.activation(out=root[1][:, blk[b]], in_=zb[1][b], func=ACT.Exp, scale=0.5, bias=-0.5)
         for h in range(2):
-            nc.scalar.activation(out=root[h][:], in_=zb[h][:], func=ACT.Exp, scale=0.5, bias=-0.5 * h)
             for b in range(MB):
-                cols = slice(b * HALF, (b + 1) * HALF)
                 nc.vector.scalar_tensor_tensor(
-                    out=res[h][:, cols], in0=hb[h][:, cols], scalar=wgt[:, b : b + 1], in1=root[h][:, cols],
+                    out=res[h][:, blk[b]], in0=hb[h][b], scalar=wgt[:, b : b + 1], in1=root[h][:, blk[b]],
                     op0=ALU.mult, op1=ALU.add,
                 )
-                nc.sync.dma_start(out[b * P : (b + 1) * P, h * HALF : (h + 1) * HALF], res[h][:, cols])
+                nc.sync.dma_start(out[b * P : (b + 1) * P, h * HALF : (h + 1) * HALF], res[h][:, blk[b]])

import math
from contextlib import ExitStack

import concourse.mybir as mybir
from concourse.masks import make_identity

K, T, S, N, R = 512, 1024, 512, 256, 256
FLOPS = 2 * 2 * K * S * N

F32 = mybir.dt.float32
BF16 = mybir.dt.bfloat16
I32 = mybir.dt.int32
U32 = mybir.dt.uint32
U16 = mybir.dt.uint16
U8 = mybir.dt.uint8
FP8X4 = mybir.dt.float8_e4m3fn_x4
ALU = mybir.AluOpType
ACT = mybir.ActivationFunctionType

P = 128
PACK = 4
HALF = S // 2
MB = N // P
JB = S // P
SPARE = 96
TINY = 1e-14


def tile_picked_ytroef_root_p_kernel(
    tc, x_words, x_scales, w1, w2, mcon, lfc, wor, offs, bath, out
):
    nc = tc.nc
    with ExitStack() as ctx:
        keep = ctx.enter_context(tc.tile_pool(name="keep", bufs=1))
        psum = ctx.enter_context(tc.psum_pool(name="psum", bufs=1))

        def sb(name, shape, dtype, tag=""):
            return keep.tile(shape, dtype, name=name, tag=tag, align_bytes=64)

        def bank(name, tag):
            return psum.tile([P, 2 * N], F32, name=name, tag=tag)

        offs_t = keep.tile([P, S // 16], U16, name="offs_t")
        bath_t = keep.tile([P, S // 16], U16, name="bath_t")

        one = sb("one", [P, 1], F32)
        shift = sb("shift", [P, 1], F32)
        nc.vector.memset(one[:], 1.0)
        nc.scalar.activation(out=shift[:], in_=one[:], func=ACT.Ln, scale=math.exp(-0.4))

        conc = sb("conc", [P, MB * R + SPARE], F32)
        scale_win = sb("scale_win", [P, T], U8)
        nc.gpsimd.memset(scale_win[:].bitcast(I32), 0)
        nc.gpsimd.memset(conc[:, MB * R :], 0.0)
        ident = sb("ident", [P, P], F32)
        make_identity(nc, ident[:])

        word_win = sb("word_win", [P, T], I32)
        w_raw = [sb("w_raw%d" % i, [P, PACK, N], F32)[:] for i in range(2)]
        cen = sb("cen", [P, JB], F32)
        wgt = sb("wgt", [P, MB], F32)

        nc.sync.dma_start(
            conc[:, : MB * R].rearrange("p (b r) -> p b r", b=MB), mcon.rearrange("(b p) r -> p b r", p=P)
        )
        nc.sync.dma_start(bath_t[:], bath)
        for q in range(4):
            nc.sync.dma_start(
                scale_win[32 * q : 32 * q + 4, :].bitcast(I32), x_scales[0, 4 * q : 4 * q + 4, :].bitcast(I32)
            )
        nc.sync.dma_start(w_raw[0], w1.rearrange("(p t) n -> p t n", t=PACK))
        nc.sync.dma_start(word_win[:], x_words[0].rearrange("p c r -> p (c r)").bitcast(I32))
        nc.sync.dma_start(offs_t[:], offs)
        nc.sync.dma_start(w_raw[1], w2.rearrange("(p t) n -> p t n", t=PACK))
        with nc.allow_non_contiguous_dma(reason="one value a partition"):
            nc.sync.dma_start(cen[:], lfc[0, :].rearrange("(b p) -> p b", p=P))
            nc.sync.dma_start(wgt[:], wor.rearrange("(b p) o -> p (b o)", p=P))

        w_codes = [sb("w_codes%d" % i, [P, N], U32) for i in range(2)]
        w_scales = [sb("w_scales%d" % i, [P, N], U8) for i in range(2)]
        w_bf = [sb("w_bf%d" % i, [P, N, PACK], BF16, "woven%d" % i) for i in range(2)]

        def weave(i):
            nc.scalar.copy(
                out=w_bf[i][:].rearrange("p (c i) t -> p c t i", i=4),
                in_=w_raw[i].rearrange("p t (c i) -> p c t i", i=4),
            )

        weave(0)
        lt = w_raw[0]
        picked = [[sb("picked%d_%d" % (b, h), [P, HALF], F32) for h in range(2)] for b in range(MB)]
        for b in range(MB):
            for h in range(2):
                nc.vector.tensor_copy(out=picked[b][h][:], in_=conc[:, b * R : (b + 1) * R + SPARE].indirect(bath_t[:, 16 * h : 16 * h + 16]))
        for b in range(MB):
            turned = bank("turned%d" % b, "a%d" % b)
            for jb in range(JB):
                nc.tensor.transpose(
                    turned[:, jb * P : (jb + 1) * P], picked[b][jb // 2][:, (jb % 2) * P : (jb % 2 + 1) * P], ident[:]
                )
            nc.scalar.activation(
                out=lt[:, :, b * P : (b + 1) * P],
                in_=turned[:].rearrange("p (j m) -> p j m", j=JB),
                func=ACT.Ln,
                scale=math.exp(-0.4),
            )

        weave(1)
        x_codes, x_bytes = [], []

        def pick_words(h, tag):
            x_codes.append(sb("x_codes%d" % h, [P, HALF], U32, tag))
            nc.vector.tensor_copy(
                out=x_codes[h][:], in_=word_win[:].bitcast(U32).indirect(offs_t[:, 16 * h : 16 * h + 16])
            )

        def pick_bytes(h, tag):
            x_bytes.append(sb("x_bytes%d" % h, [P, HALF], U8, tag))
            nc.vector.tensor_copy(out=x_bytes[h][:], in_=scale_win[:].indirect(offs_t[:, 16 * h : 16 * h + 16]))

        def quantise(i):
            nc.vector.quantize_mx(
                out=w_codes[i][:].bitcast(FP8X4), scales=w_scales[i][:], in_=w_bf[i][:].rearrange("p n t -> p (n t)")
            )

        pick_words(0, "")
        pick_bytes(0, "")
        quantise(0)
        pick_words(1, "woven0")
        pick_bytes(1, "")
        quantise(1)

        y = [[bank("y%d_%d" % (i, h), "y%d_%d" % (i, h)) for h in range(2)] for i in range(2)]
        for i in range(2):
            for h in range(2):
                for jl in range(2):
                    cols = slice(jl * P, (jl + 1) * P)
                    nc.tensor.matmul_mx(
                        out=y[i][h][:, jl * N : (jl + 1) * N],
                        lhsT=x_codes[h][:, cols].bitcast(FP8X4),
                        lhsT_scale=x_bytes[h][:, cols],
                        rhs=w_codes[i][:].bitcast(FP8X4),
                        rhs_scale=w_scales[i][:],
                        start=True,
                        stop=True,
                    )

        wid2 = sb("wid2", [P, JB], F32)
        nc.scalar.activation(out=wid2[:], in_=cen[:], func=ACT.Square, scale=-0.5, bias=1.0)

        def halves(name):
            return [sb("%s%d" % (name, h), [P, 2 * N], F32) for h in range(2)]

        low, gap, far, lfar, lmin, near = (halves(n) for n in ("low", "gap", "far", "lfar", "lmin", "near"))
        lf = [lfar[1], lfar[0]]
        side = sb("side", [P, 4 * N + 8], F32)
        sq, cw2, farm = side[:, : 2 * N], side[:, 2 * N : 2 * N + JB], side[:, 2 * N + 8 :]
        sq0 = [side[:, 3 * N // 2 : 5 * N // 2], side[:, :N]]
        den = sb("den", [P, 2 * N], F32)
        lden = sb("lden", [P, 2 * N], F32)
        rec = sb("rec", [P, 2 * N], F32)
        root = [lden, sb("root1", [P, 2 * N], F32)]
        res = [rec, sb("res1", [P, 2 * N], F32)]
        pair = sb("pair", [P, N], F32)
        inv = sb("inv", [P, N], F32)
        blk = [slice(jl * N, (jl + 1) * N) for jl in range(2)]

        for h in range(2):
            nc.vector.scalar_tensor_tensor(
                out=low[h][:], in0=y[0][h][:], scalar=0.8,
                in1=lt[:, 2 * h : 2 * h + 2, :].rearrange("p j m -> p (j m)"), op0=ALU.mult, op1=ALU.add,
            )
        for h, cols in ((0, slice(0, 2 * N)), (1, blk[0]), (1, blk[1])):
            nc.vector.scalar_tensor_tensor(
                out=gap[h][:, cols], in0=y[1][h][:, cols], scalar=0.8, in1=low[h][:, cols],
                op0=ALU.mult, op1=ALU.subtract,
            )
            nc.scalar.activation(out=far[h][:, cols], in_=gap[h][:, cols], func=ACT.Sigmoid, bias=shift[:])

        for jl in (1, 0):
            nc.vector.tensor_tensor(
                out=sq0[jl], in0=gap[0][:, blk[jl]], in1=gap[0][:, blk[jl]], op=ALU.mult
            )
        for jl in (1, 0):
            nc.vector.tensor_scalar(
                out=den[:, blk[jl]], in0=sq0[jl], scalar1=wid2[:, jl : jl + 1], scalar2=None, op0=ALU.add
            )
        nc.vector.scalar_tensor_tensor(
            out=pair[:], in0=sq0[0], scalar=wid2[:, 0:1], in1=den[:, blk[1]], op0=ALU.add, op1=ALU.mult
        )
        nc.vector.reciprocal(out=inv[:], in_=pair[:])
        nc.gpsimd.tensor_tensor(out=sq, in0=gap[1][:], in1=gap[1][:], op=ALU.mult)
        nc.gpsimd.tensor_tensor(out=cw2, in0=wid2[:], in1=cen[:], op=ALU.mult)
        nc.gpsimd.tensor_scalar(out=farm, in0=far[0][:], scalar1=1.0, scalar2=-1.0, op0=ALU.mult, op1=ALU.add)

        for h in range(2):
            nc.scalar.activation(out=lfar[h][:], in_=far[h][:], func=ACT.Ln, scale=math.exp(0.4), bias=TINY)
        for jl in range(2):
            nc.scalar.activation(
                out=lden[:, blk[jl]], in_=sq[:, blk[jl]], func=ACT.Ln, bias=wid2[:, 2 + jl : 3 + jl]
            )
        for jl in range(2):
            nc.scalar.activation(out=rec[:, blk[jl]], in_=lden[:, blk[jl]], func=ACT.Exp, scale=-1.0)

        z0, h0 = bank("z0", "z0"), bank("h0", "a0")
        zb = [[z0[:, blk[b]] for b in range(MB)], [bank("z1_%d" % b, t)[:, :HALF] for b, t in enumerate(("z1", "a1"))]]
        hb = [[h0[:, blk[b]] for b in range(MB)], [bank("h1_%d" % b, "y0_%d" % b)[:, :HALF] for b in range(MB)]]

        def turn(dst, h, src, first, last):
            for jl in range(2):
                for b in range(MB):
                    opens = jl == 0 and (h == 1 or b == 0)
                    closes = jl == 1 and (h == 1 or b == MB - 1)
                    nc.tensor.matmul(
                        out=dst[h][b][:, jl * P : (jl + 1) * P],
                        lhsT=src[:, jl * N + b * P : jl * N + (b + 1) * P],
                        rhs=ident[:],
                        is_transpose=True,
                        start=first and opens,
                        stop=last and closes,
                    )

        for h in range(2):
            turn(zb, h, low[h], True, False)
        for h in range(2):
            nc.vector.tensor_tensor(out=lmin[h][:], in0=lfar[h][:], in1=gap[h][:], op=ALU.min)
            turn(zb, h, lmin[h], False, False)
        for jl in range(2):
            nc.vector.scalar_tensor_tensor(
                out=lf[0][:, blk[jl]], in0=inv[:], scalar=cw2[:, jl : jl + 1], in1=den[:, blk[1 - jl]],
                op0=ALU.mult, op1=ALU.mult,
            )
        turn(zb, 0, lf[0], False, True)
        for jl in range(2):
            nc.vector.scalar_tensor_tensor(
                out=near[0][:, blk[jl]], in0=lf[0][:, blk[jl]], scalar=1.0, in1=farm[:, blk[jl]],
                op0=ALU.add, op1=ALU.mult,
            )
        turn(hb, 0, near[0], True, True)
        for jl in range(2):
            nc.vector.tensor_scalar(
                out=lf[1][:, blk[jl]], in0=rec[:, blk[jl]], scalar1=cw2[:, 2 + jl : 3 + jl], scalar2=1.0,
                op0=ALU.mult, op1=ALU.add,
            )
        turn(zb, 1, lf[1], False, True)
        for jl in range(2):
            nc.vector.scalar_tensor_tensor(
                out=near[1][:, blk[jl]], in0=far[1][:, blk[jl]], scalar=1.0, in1=lf[1][:, blk[jl]],
                op0=ALU.subtract, op1=ALU.mult,
            )
        turn(hb, 1, near[1], True, True)

        nc.scalar.activation(out=root[0][:], in_=z0[:], func=ACT.Exp, scale=0.5)
        for b in range(MB):
            nc.scalar.activation(out=root[1][:, blk[b]], in_=zb[1][b], func=ACT.Exp, scale=0.5, bias=-0.5)
        for h in range(2):
            for b in range(MB):
                nc.vector.scalar_tensor_tensor(
                    out=res[h][:, blk[b]], in0=hb[h][b], scalar=wgt[:, b : b + 1], in1=root[h][:, blk[b]],
                    op0=ALU.mult, op1=ALU.add,
                )
                nc.sync.dma_start(out[b * P : (b + 1) * P, h * HALF : (h + 1) * HALF], res[h][:, blk[b]])
